import numpy as np
import ml_dtypes


def mxq(x, axis, fmt="e4m3"):
    dtype, down = {"e4m3": (ml_dtypes.float8_e4m3fn, 7), "e5m2": (ml_dtypes.float8_e5m2, 14)}[fmt]
    v = np.moveaxis(np.asarray(x, np.float32).astype(ml_dtypes.bfloat16).astype(np.float64), axis, -1)
    blocks = v.reshape(v.shape[:-1] + (-1, 32))
    amax = np.abs(blocks).max(-1, keepdims=True)
    byte = np.maximum(np.where(amax > 0, np.frexp(amax)[1] - 1 + 127, 0) - down, 1)
    scale = np.exp2(byte - 127.0)
    codes = (blocks / scale).astype(np.float32).astype(dtype).astype(np.float64)
    return np.moveaxis((codes * scale).reshape(v.shape), -1, axis)


WIDE = False


def mx_kscale(k):
    if not WIDE:
        return np.ones(k)
    levels = np.array([10, -10, 5, -5, 0])
    if k % 512:
        return np.exp2(np.random.permutation(np.resize(levels, k // 32))).repeat(32)
    a = np.empty((k // 512, 16))
    for p in range(k // 512):
        a[p, :8] = np.random.permutation(np.resize(levels, 8))
        for g in range(8):
            far = levels[np.abs(levels - a[p, g]) >= 10]
            a[p, g + 8] = far[np.random.randint(len(far))]
    return np.exp2(a.ravel()).repeat(32)


def f64(x):
    return np.asarray(x).astype(np.float64)


def striped(idx):
    return np.tile(idx.reshape(-1, 16).T, (8, 1)).astype(np.uint16)


def unstriped(offs):
    return offs[:16].T.reshape(-1).astype(np.int64)


def pack_weight(w):
    k, n = w.shape
    w = f64(np.asarray(w, np.float32).astype(ml_dtypes.bfloat16)).reshape(k // 32, 32, n)
    amax = np.abs(w).max(1)
    byte = np.clip(np.where(amax > 0, np.frexp(amax)[1] - 1 + 127 - 7, 1), 1, 254)
    scaled = (w * np.exp2(127.0 - byte)[:, None, :]).reshape(k, n).astype(np.float32)
    words = np.ascontiguousarray(scaled.reshape(k // 512, 128, 4, n).transpose(0, 1, 3, 2)).astype(ml_dtypes.float8_e4m3fn).view(np.uint8)
    return words, np.ascontiguousarray(byte.astype(np.uint8).reshape(k // 512, 16, n))


def unpack_weight(words, scales):
    g, p, n, _ = words.shape
    vals = np.ascontiguousarray(words).view(ml_dtypes.float8_e4m3fn).astype(np.float64) * np.repeat(np.exp2(scales.astype(np.float64) - 127.0), 8, axis=1)[..., None]
    return vals.transpose(0, 1, 3, 2).reshape(g * 512, n)


E2M1 = np.array([0.0, 0.5, 1.0, 1.5, 2.0, 3.0, 4.0, 6.0, -0.0, -0.5, -1.0, -1.5, -2.0, -3.0, -4.0, -6.0])


def pack_fp4(w):
    k, n = w.shape
    w = f64(np.asarray(w, np.float32).astype(ml_dtypes.bfloat16)).reshape(k // 32, 32, n)
    amax = np.abs(w).max(1)
    mant, ex = np.frexp(amax / 6.0)
    byte = np.clip(np.where(amax > 0, np.where(mant > 0.5, ex, ex - 1) + 127, 1), 1, 254)
    scaled = (w * np.exp2(127.0 - byte)[:, None, :]).reshape(k, n).astype(np.float32)
    c = np.ascontiguousarray(scaled.reshape(k // 512, 128, 4, n).transpose(0, 1, 3, 2)).astype(ml_dtypes.float4_e2m1fn).view(np.uint8) & 0xF
    words = (c[..., 0::2] | (c[..., 1::2] << 4)).reshape(k // 512, 128, 2 * n)
    return np.ascontiguousarray(words), np.ascontiguousarray(byte.astype(np.uint8).reshape(k // 512, 16, n))


def unpack_fp4(words, scales):
    g, _, n = scales.shape
    words = np.ascontiguousarray(words).reshape(g, 128, n, 2)
    nib = np.empty((g, 128, n, 4), np.uint8)
    nib[..., 0::2] = words & 0xF
    nib[..., 1::2] = words >> 4
    vals = E2M1[nib] * np.repeat(np.exp2(scales.astype(np.float64) - 127.0), 8, axis=1)[..., None]
    return vals.transpose(0, 1, 3, 2).reshape(g * 512, n)


def planes(y):
    n, m = y.shape
    v = y.astype(np.float32).astype(ml_dtypes.bfloat16).astype(np.float64).reshape(n // 32, 32, m)
    top = np.abs(v).max(1)
    byte = np.clip(np.where(top > 0, np.frexp(top)[1] - 1 + 127 - 7, 1), 1, 254)
    codes = (v * np.exp2(127.0 - byte)[:, None, :]).reshape(n, m).astype(np.float32).astype(ml_dtypes.float8_e4m3fn).view(np.uint8)
    words = codes.reshape(n // 512, 128, 4, m).transpose(0, 1, 3, 2)
    return np.ascontiguousarray(words), np.ascontiguousarray(byte.astype(np.uint8).reshape(n // 512, 16, m))


K, T, S, N, H, W, C = 512, 2048, 512, 512, 512, 2048, 512


def setup_inputs():
    n = np.random.standard_normal
    s = mx_kscale(K)[:, None]
    u = mx_kscale(S)
    packed_xT = pack_weight(n((K, T)) * s)
    packed_w1 = pack_fp4(n((K, H)) / np.sqrt(K) / s)
    packed_w2 = pack_fp4(n((H, N)) / np.sqrt(H) / u[:, None])
    return {
        "x_words": packed_xT[0],
        "x_scales": packed_xT[1],
        "w1_words": packed_w1[0],
        "w1_scales": packed_w1[1],
        "gn": (np.random.uniform(0.5, 1.5, (H, 1)) * u[:, None]).astype(np.float32),
        "w2_words": packed_w2[0],
        "w2_scales": packed_w2[1],
        "gs": (np.random.uniform(0.5, 1.5, (K, 1)) / s).astype(np.float32),
        "offs": striped(np.random.permutation(T)[:S]),
        "n1": striped(np.random.permutation(S)),
        "n2": striped(np.random.permutation(S)),
        "n3": striped(np.random.randint(0, S, W)),
        "cand": striped(np.random.permutation(T)[:C]),
        "n4": striped(np.random.permutation(S)),
        "n5": striped(np.random.permutation(S)),
    }


def reference(x_words, x_scales, w1_words, w1_scales, gn, w2_words, w2_scales, gs, offs, n1, n2, n3, cand, n4, n5):
    xq = unpack_weight(x_words, x_scales)[:, unstriped(offs)]
    y = unpack_fp4(w1_words, w1_scales).T @ xq
    z = f64(gn) * (y[:, unstriped(n1)] - y[:, unstriped(n2)])
    a = unpack_fp4(w2_words, w2_scales).T @ mxq(z, 0, "e4m3")
    x_cand = unpack_weight(x_words, x_scales)[:, unstriped(cand)]
    mb = y[:, unstriped(n3)]
    mn = mb.reshape(H, S, 4).min(axis=2)
    mx = mb.reshape(H, S, 4).max(axis=2)
    z2 = f64(gs) * (np.maximum(y, mn) - (0.5 * mx))
    b = 0.0625 * ((x_cand.T @ mxq(z2, 0, "e4m3")))
    out_0 = (a - a[:, unstriped(n4)]) / (np.abs(b) + np.abs(b[:, unstriped(n5)]) + 0.5)
    return (out_0,) + planes(out_0)

@@ -1,0 +1,247 @@
+from contextlib import ExitStack
+
+import concourse.mybir as mybir
+
+K, T, S, H, N, C, MEMBERS = 512, 2048, 512, 512, 512, 512, 4
+FLOPS = 2 * K * H * S + 2 * H * N * S + 2 * K * C * S
+
+F32 = mybir.dt.float32
+BF16 = mybir.dt.bfloat16
+I32 = mybir.dt.int32
+U32 = mybir.dt.uint32
+U16 = mybir.dt.uint16
+U8 = mybir.dt.uint8
+FP8X4 = mybir.dt.float8_e4m3fn_x4
+FP4X4 = mybir.dt.float4_e2m1fn_x4
+ALU = mybir.AluOpType
+ACT = mybir.ActivationFunctionType
+
+P = 128
+PACK = 4
+LANES = 16
+SPARE = 16
+HALF = S // 2
+CHUNK = 128
+N5_ON_VECTOR = 2
+N4_ON_VECTOR = 1
+FIRST_ON_VECTOR = 1
+
+
+def tile_picked_fkcdnormbgapgmid_none_po_kernel(
+    tc, x_words, x_scales, w1_words, w1_scales, gn, w2_words, w2_scales, gs, offs, n1, n2, n3, cand, n4, n5, out_0, out_1, out_2
+):
+    nc = tc.nc
+    with ExitStack() as ctx:
+        keep = ctx.enter_context(tc.tile_pool(name="keep", bufs=1))
+        ring = ctx.enter_context(tc.tile_pool(name="ring", bufs=2))
+        psum = ctx.enter_context(tc.psum_pool(name="psum", bufs=8))
+
+        def load_list(src, name):
+            lst = keep.tile([P, src.shape[1]], U16, name=name)
+            nc.sync.dma_start(lst[:], src)
+            return lst
+
+        def load_scales(src, name, clearers, queue):
+            width = src.shape[2]
+            plane = keep.tile([P, width], U8, name=name, align_bytes=64)
+            share = width // len(clearers)
+            for e, engine in enumerate(clearers):
+                engine.memset(plane[:, share * e : share * (e + 1)].bitcast(I32), 0)
+            for q in range(4):
+                queue.dma_start(plane[32 * q : 32 * q + 4, :].bitcast(I32), src[0, 4 * q : 4 * q + 4, :].bitcast(I32))
+            return plane
+
+        def load_words(src2d, name, queue):
+            raw = keep.tile([P, src2d.shape[1]], U8, name=name, align_bytes=64)
+            queue.dma_start(raw[:].bitcast(I32), src2d.bitcast(I32))
+            return raw
+
+        def load_gain(src, name):
+            gain = keep.tile([P, PACK], F32, name=name)
+            nc.sync.dma_start(gain[:], src.rearrange("(p t) o -> p (t o)", t=PACK))
+            return gain
+
+        def deal(engine, src, name, dtype, unit, run):
+            dealt = keep.tile([P, src.shape[1]], dtype, name=name, align_bytes=64)
+            engine.tensor_copy(
+                dealt[:].rearrange("p (t c i b) -> p c t i b", t=PACK, i=run, b=unit),
+                src.rearrange("p (c i t b) -> p c t i b", t=PACK, i=run, b=unit),
+            )
+            return dealt
+
+        def entries(lst, first, count):
+            return lst[:, first // LANES : (first + count) // LANES]
+
+        offs_l = load_list(offs, "offs_l")
+        cand_l = load_list(cand, "cand_l")
+        w1_raw = load_words(w1_words[0], "w1_raw", nc.sync)
+        xs = load_scales(x_scales, "xs", (nc.vector, nc.gpsimd), nc.scalar)
+        xw = keep.tile([P, T], I32, name="xw", align_bytes=64)
+        nc.sync.dma_start(xw[:], x_words[0].rearrange("p n t -> p (n t)").bitcast(I32))
+        w1s_raw = load_scales(w1_scales, "w1s_raw", (nc.gpsimd,), nc.scalar)
+        n3_l = load_list(n3, "n3_l")
+        n2_l = load_list(n2, "n2_l")
+        n1_l = load_list(n1, "n1_l")
+        gs_t = load_gain(gs, "gs_t")
+        gn_t = load_gain(gn, "gn_t")
+        w2_raw = load_words(w2_words[0], "w2_raw", nc.sync)
+        w2s_raw = load_scales(w2_scales, "w2s_raw", (nc.gpsimd,), nc.sync)
+        n4_l = load_list(n4, "n4_l")
+        n5_l = load_list(n5, "n5_l")
+
+        y = [keep.tile([P, S + SPARE], F32, name=f"y{t}") for t in range(PACK)]
+        for t in range(PACK):
+            nc.gpsimd.memset(y[t][:, S:], 0.0)
+
+        w1_q = deal(nc.vector, w1_raw[:], "w1_q", U8, 2, 8)
+        xq_s = keep.tile([P, S], U8, name="xq_s", align_bytes=64)
+        nc.vector.tensor_copy(xq_s[:], xs[:].indirect(offs_l[:]))
+        xc_s_raw = keep.tile([P, C], U8, name="xc_s_raw", align_bytes=64)
+        nc.vector.tensor_copy(xc_s_raw[:], xs[:].indirect(cand_l[:]))
+        xc_s = deal(nc.vector, xc_s_raw[:], "xc_s", U8, 1, 16)
+        xq = keep.tile([P, S], U32, name="xq", align_bytes=64)
+        nc.vector.tensor_copy(xq[:], xw[:].bitcast(U32).indirect(offs_l[:]))
+        w1_s = deal(nc.gpsimd, w1s_raw[:], "w1_s", U8, 1, 16)
+        w2_q = deal(nc.gpsimd, w2_raw[:], "w2_q", U8, 2, 8)
+        w2_s = deal(nc.gpsimd, w2s_raw[:], "w2_s", U8, 1, 16)
+
+        def product(t, lhs, lhs_s, rhs, rhs_s):
+            acc = psum.tile([P, S], F32, name="acc")
+            nc.tensor.matmul_mx(acc[:], lhsT=lhs, lhsT_scale=lhs_s[:, P * t : P * (t + 1)], rhs=rhs[:].bitcast(FP8X4), rhs_scale=rhs_s[:], start=True, stop=True)
+            return acc
+
+        def fp4_cols(w, t):
+            return w[:, 2 * P * t : 2 * P * (t + 1)].bitcast(FP4X4)
+
+        for t in range(PACK):
+            acc = product(t, fp4_cols(w1_q, t), w1_s, xq, xq_s)
+            if t == 0:
+                nc.scalar.copy(y[t][:, :S], acc[:])
+            else:
+                nc.vector.tensor_copy(y[t][:, :S], acc[:])
+
+        def scalar_gather(dst, window, offsets):
+            nc.scalar.activation(dst, window.indirect(offsets), ACT.Copy)
+
+        def vector_gather(dst, window, offsets):
+            nc.vector.tensor_copy(dst, window.indirect(offsets))
+
+        def fetch_members(t):
+            mb = keep.tile([P, S, MEMBERS], F32, name=f"mb{t}")
+            flat = mb[:].rearrange("p j m -> p (j m)")
+            for piece in range(MEMBERS):
+                gather = vector_gather if t == 0 and piece >= MEMBERS - FIRST_ON_VECTOR else scalar_gather
+                gather(flat[:, S * piece : S * (piece + 1)], y[t][:], entries(n3_l, S * piece, S))
+            return mb
+
+        u = keep.tile([P, PACK, S], F32, name="u")
+        d = u
+        lo = keep.tile([P, S, 2], F32, name="lo", align_bytes=64)
+        hi = keep.tile([P, S, 2], F32, name="hi", align_bytes=64)
+        mn = keep.tile([P, S], F32, name="mn")
+        mx = keep.tile([P, S], F32, name="mx")
+        top = keep.tile([P, S], F32, name="top")
+
+        def extremes(t, mb):
+            nc.vector.tensor_tensor(lo[:], mb[:, :, 0:2], mb[:, :, 2:4], ALU.min)
+            nc.vector.tensor_tensor(hi[:], mb[:, :, 0:2], mb[:, :, 2:4], ALU.max)
+            nc.vector.tensor_tensor(mn[:], lo[:, :, 0], lo[:, :, 1], ALU.min)
+            nc.vector.tensor_tensor(mx[:], hi[:, :, 0], hi[:, :, 1], ALU.max)
+            nc.vector.tensor_tensor(top[:], mn[:], y[t][:, :S], ALU.max)
+
+        def combine(t):
+            nc.vector.scalar_tensor_tensor(u[:, t, :], mx[:], -0.5, top[:], ALU.mult, ALU.add)
+
+        def walk_src(ap):
+            return ap.rearrange("p t (c i) -> p c t i", i=2)
+
+        def walk_dst(ap):
+            return ap.rearrange("p (c i t) -> p c t i", i=2, t=PACK)
+
+        def quantise(vals, gain, name):
+            codes = keep.tile([P, S], U32, name=name + "_q", align_bytes=64)
+            scales = keep.tile([P, S], U8, name=name + "_s", align_bytes=64)
+            factor = gain[:].unsqueeze(1).unsqueeze(3).to_broadcast([P, HALF // 2, PACK, 2])
+            rounded = [pairs[:].rearrange("p j m -> p (j m)").bitcast(BF16)[:, : HALF * PACK] for pairs in (lo, hi)]
+            for h in range(2):
+                nc.vector.tensor_tensor(walk_dst(rounded[h]), walk_src(vals[:, :, HALF * h : HALF * (h + 1)]), factor, ALU.mult)
+            for h in range(2):
+                cols = slice(HALF * h, HALF * (h + 1))
+                nc.vector.quantize_mx(codes[:, cols].bitcast(FP8X4), scales[:, cols], rounded[h])
+            return codes, scales
+
+        mb0 = fetch_members(0)
+        xc_raw = keep.tile([P, C], U32, name="xc_raw", align_bytes=64)
+        nc.vector.tensor_copy(xc_raw[:], xw[:].bitcast(U32).indirect(cand_l[:]))
+        xc = deal(nc.vector, xc_raw[:].bitcast(I32), "xc", I32, 1, 4)
+
+        at_n2 = keep.tile([P, PACK, S], F32, name="at_n2")
+        at_n1 = keep.tile([P, PACK, S], F32, name="at_n1")
+
+        def half_list(lst, cols):
+            return entries(lst, cols.start, cols.stop - cols.start)
+
+        mb = mb0
+        for t in range(PACK):
+            ahead = fetch_members(t + 1) if t + 1 < PACK else None
+            extremes(t, mb)
+            combine(t)
+            mb = ahead
+        for t in range(PACK):
+            scalar_gather(at_n2[:, t, :], y[t][:], n2_l[:])
+            scalar_gather(at_n1[:, t, :], y[t][:], n1_l[:])
+        z2_q, z2_s = quantise(u, gs_t, "z2")
+
+        size = keep.tile([P, PACK, S], F32, name="size")
+        for t in range(PACK):
+            acc = product(t, xc[:, P * t : P * (t + 1)].bitcast(FP8X4), xc_s, z2_q, z2_s)
+            nc.scalar.activation(size[:, t, :], acc[:], ACT.Abs, scale=0.0625)
+        for t in range(PACK):
+            nc.vector.tensor_tensor(d[:, t, :], at_n1[:, t, :], at_n2[:, t, :], ALU.subtract)
+        z_q, z_s = quantise(d, gn_t, "z")
+
+        out_rows = out_0.rearrange("(p t) j -> p t j", t=PACK)
+        codes = keep.tile([P, S], U32, name="codes", align_bytes=64)
+        scales = keep.tile([P, S], U8, name="scales", align_bytes=64)
+        out_words = out_1[0].rearrange("p j t -> p (j t)").bitcast(I32)
+        chunks = [slice(c, c + CHUNK) for c in range(0, S, CHUNK)]
+
+        at_n5 = keep.tile([P, PACK, S], F32, name="at_n5")
+        for cols in chunks:
+            for t in range(PACK):
+                gather = vector_gather if t < N5_ON_VECTOR else scalar_gather
+                gather(at_n5[:, t, cols], size[:, t, :], half_list(n5_l, cols))
+        a = keep.tile([P, PACK, S], F32, name="a")
+        for t in range(PACK):
+            acc = product(t, fp4_cols(w2_q, t), w2_s, z_q, z_s)
+            nc.scalar.copy(a[:, t, :], acc[:])
+
+        def parts(cols):
+            den = ring.tile([P, PACK, CHUNK], F32, name="den")
+            nc.vector.tensor_tensor(den[:], at_n5[:, :, cols], size[:, :, cols], ALU.add)
+            at_n4 = ring.tile([P, PACK, CHUNK], F32, name="at_n4")
+            for t in range(PACK):
+                gather = vector_gather if t < N4_ON_VECTOR else scalar_gather
+                gather(at_n4[:, t, :], a[:, t, :], half_list(n4_l, cols))
+            root = ring.tile([P, PACK, CHUNK], F32, name="root")
+            nc.scalar.activation(root[:], den[:], ACT.Abs_reciprocal_sqrt, bias=0.5)
+            inv = ring.tile([P, PACK, CHUNK], F32, name="inv")
+            nc.scalar.activation(inv[:], root[:], ACT.Square)
+            num = ring.tile([P, PACK, CHUNK], F32, name="num")
+            nc.vector.tensor_tensor(num[:], a[:, :, cols], at_n4[:], ALU.subtract)
+            return num, inv
+
+        def finish(cols, num, inv):
+            res = keep.tile([P, PACK, CHUNK], F32, name=f"res{cols.start}")
+            nc.vector.tensor_tensor(res[:], num[:], inv[:], ALU.mult)
+            nc.sync.dma_start(out_rows[:, :, cols], res[:])
+            grouped = ring.tile([P, CHUNK * PACK], BF16, name="grouped", align_bytes=64)
+            nc.vector.tensor_copy(walk_dst(grouped[:]), walk_src(res[:]))
+            nc.vector.quantize_mx(codes[:, cols].bitcast(FP8X4), scales[:, cols], grouped[:])
+            nc.sync.dma_start(out_words[:, cols], codes[:, cols].bitcast(I32))
+
+        for cols in chunks:
+            finish(cols, *parts(cols))
+        for q in range(4):
+            queue = nc.sync if q % 2 == 0 else nc.scalar
+            queue.dma_start(out_2[0, 4 * q : 4 * q + 4, :].bitcast(I32), scales[32 * q : 32 * q + 4, :].bitcast(I32))

@@ -21,10 +21,12 @@ PACK = 4
 LANES = 16
 SPARE = 16
 HALF = S // 2
-CHUNK = 128
-N5_ON_VECTOR = 2
-N4_ON_VECTOR = 1
-FIRST_ON_VECTOR = 1
+WIDTHS = (128, 128, 128, 128)
+A_ON_SCALAR = 0
+LEAD = 1
+N5_ON_VECTOR = (4, 0, 0, 0)
+N4_ON_VECTOR = (4, 0, 0, 0)
+MEMBERS_ON_VECTOR = (2, 0, 0, 0)
 
 
 def tile_picked_fkcdnormbgapgmid_none_po_kernel(
@@ -51,6 +53,14 @@ def tile_picked_fkcdnormbgapgmid_none_po_kernel(
                 queue.dma_start(plane[32 * q : 32 * q + 4, :].bitcast(I32), src[0, 4 * q : 4 * q + 4, :].bitcast(I32))
             return plane
 
+        def load_scales_everywhere(src, name):
+            width = src.shape[2]
+            plane = keep.tile([P, width], U8, name=name, align_bytes=64)
+            for q in range(4):
+                rows = src[0, 4 * q : 4 * q + 4, :].bitcast(I32).unsqueeze(0).to_broadcast([8, 4, width // 4])
+                nc.sync.dma_start(plane[32 * q : 32 * q + 32, :].bitcast(I32), rows)
+            return plane
+
         def load_words(src2d, name, queue):
             raw = keep.tile([P, src2d.shape[1]], U8, name=name, align_bytes=64)
             queue.dma_start(raw[:].bitcast(I32), src2d.bitcast(I32))
@@ -73,52 +83,57 @@ def tile_picked_fkcdnormbgapgmid_none_po_kernel(
             return lst[:, first // LANES : (first + count) // LANES]
 
         offs_l = load_list(offs, "offs_l")
-        cand_l = load_list(cand, "cand_l")
+        xs = load_scales_everywhere(x_scales, "xs")
         w1_raw = load_words(w1_words[0], "w1_raw", nc.sync)
-        xs = load_scales(x_scales, "xs", (nc.vector, nc.gpsimd), nc.scalar)
+        cand_l = load_list(cand, "cand_l")
         xw = keep.tile([P, T], I32, name="xw", align_bytes=64)
         nc.sync.dma_start(xw[:], x_words[0].rearrange("p n t -> p (n t)").bitcast(I32))
-        w1s_raw = load_scales(w1_scales, "w1s_raw", (nc.gpsimd,), nc.scalar)
+        w1s_raw = load_scales(w1_scales, "w1s_raw", (nc.gpsimd,), nc.sync)
         n3_l = load_list(n3, "n3_l")
-        n2_l = load_list(n2, "n2_l")
-        n1_l = load_list(n1, "n1_l")
-        gs_t = load_gain(gs, "gs_t")
         gn_t = load_gain(gn, "gn_t")
         w2_raw = load_words(w2_words[0], "w2_raw", nc.sync)
         w2s_raw = load_scales(w2_scales, "w2s_raw", (nc.gpsimd,), nc.sync)
-        n4_l = load_list(n4, "n4_l")
+        n2_l = load_list(n2, "n2_l")
+        n1_l = load_list(n1, "n1_l")
+        gs_t = load_gain(gs, "gs_t")
         n5_l = load_list(n5, "n5_l")
+        n4_l = load_list(n4, "n4_l")
 
         y = [keep.tile([P, S + SPARE], F32, name=f"y{t}") for t in range(PACK)]
         for t in range(PACK):
             nc.gpsimd.memset(y[t][:, S:], 0.0)
 
-        w1_q = deal(nc.vector, w1_raw[:], "w1_q", U8, 2, 8)
+        w1_q = deal(nc.gpsimd, w1_raw[:], "w1_q", U8, 2, 8)
         xq_s = keep.tile([P, S], U8, name="xq_s", align_bytes=64)
         nc.vector.tensor_copy(xq_s[:], xs[:].indirect(offs_l[:]))
         xc_s_raw = keep.tile([P, C], U8, name="xc_s_raw", align_bytes=64)
         nc.vector.tensor_copy(xc_s_raw[:], xs[:].indirect(cand_l[:]))
-        xc_s = deal(nc.vector, xc_s_raw[:], "xc_s", U8, 1, 16)
         xq = keep.tile([P, S], U32, name="xq", align_bytes=64)
-        nc.vector.tensor_copy(xq[:], xw[:].bitcast(U32).indirect(offs_l[:]))
+        for first in (0, HALF):
+            nc.vector.tensor_copy(xq[:, first : first + HALF], xw[:].bitcast(U32).indirect(entries(offs_l, first, HALF)))
         w1_s = deal(nc.gpsimd, w1s_raw[:], "w1_s", U8, 1, 16)
+        xc_s = deal(nc.vector, xc_s_raw[:], "w1s_raw", U8, 1, 16)
         w2_q = deal(nc.gpsimd, w2_raw[:], "w2_q", U8, 2, 8)
         w2_s = deal(nc.gpsimd, w2s_raw[:], "w2_s", U8, 1, 16)
 
-        def product(t, lhs, lhs_s, rhs, rhs_s):
-            acc = psum.tile([P, S], F32, name="acc")
-            nc.tensor.matmul_mx(acc[:], lhsT=lhs, lhsT_scale=lhs_s[:, P * t : P * (t + 1)], rhs=rhs[:].bitcast(FP8X4), rhs_scale=rhs_s[:], start=True, stop=True)
+        def product(t, lhs, lhs_s, rhs, rhs_s, cols=slice(0, S)):
+            acc = psum.tile([P, cols.stop - cols.start], F32, name="acc")
+            nc.tensor.matmul_mx(acc[:], lhsT=lhs, lhsT_scale=lhs_s[:, P * t : P * (t + 1)], rhs=rhs[:, cols].bitcast(FP8X4), rhs_scale=rhs_s[:, cols], start=True, stop=True)
             return acc
 
         def fp4_cols(w, t):
             return w[:, 2 * P * t : 2 * P * (t + 1)].bitcast(FP4X4)
 
-        for t in range(PACK):
+        for first in (0, HALF):
+            cols = slice(first, first + HALF)
+            acc = product(0, fp4_cols(w1_q, 0), w1_s, xq, xq_s, cols)
+            nc.scalar.copy(y[0][:, cols], acc[:])
+        for t in range(1, PACK):
             acc = product(t, fp4_cols(w1_q, t), w1_s, xq, xq_s)
-            if t == 0:
-                nc.scalar.copy(y[t][:, :S], acc[:])
-            else:
-                nc.vector.tensor_copy(y[t][:, :S], acc[:])
+            nc.vector.tensor_copy(y[t][:, :S], acc[:])
+        gained = [keep.tile([P, S + SPARE], F32, name=f"gained{t}") for t in range(PACK)]
+        for t in range(PACK):
+            nc.gpsimd.tensor_scalar(gained[t][:], y[t][:], gn_t[:, t : t + 1], 0.0, ALU.mult, ALU.add)
 
         def scalar_gather(dst, window, offsets):
             nc.scalar.activation(dst, window.indirect(offsets), ACT.Copy)
@@ -130,12 +145,11 @@ def tile_picked_fkcdnormbgapgmid_none_po_kernel(
             mb = keep.tile([P, S, MEMBERS], F32, name=f"mb{t}")
             flat = mb[:].rearrange("p j m -> p (j m)")
             for piece in range(MEMBERS):
-                gather = vector_gather if t == 0 and piece >= MEMBERS - FIRST_ON_VECTOR else scalar_gather
+                gather = vector_gather if piece >= MEMBERS - MEMBERS_ON_VECTOR[t] else scalar_gather
                 gather(flat[:, S * piece : S * (piece + 1)], y[t][:], entries(n3_l, S * piece, S))
             return mb
 
         u = keep.tile([P, PACK, S], F32, name="u")
-        d = u
         lo = keep.tile([P, S, 2], F32, name="lo", align_bytes=64)
         hi = keep.tile([P, S, 2], F32, name="hi", align_bytes=64)
         mn = keep.tile([P, S], F32, name="mn")
@@ -158,13 +172,13 @@ def tile_picked_fkcdnormbgapgmid_none_po_kernel(
         def walk_dst(ap):
             return ap.rearrange("p (c i t) -> p c t i", i=2, t=PACK)
 
-        def quantise(vals, gain, name):
+        def quantise(first, second, op, name):
             codes = keep.tile([P, S], U32, name=name + "_q", align_bytes=64)
             scales = keep.tile([P, S], U8, name=name + "_s", align_bytes=64)
-            factor = gain[:].unsqueeze(1).unsqueeze(3).to_broadcast([P, HALF // 2, PACK, 2])
             rounded = [pairs[:].rearrange("p j m -> p (j m)").bitcast(BF16)[:, : HALF * PACK] for pairs in (lo, hi)]
             for h in range(2):
-                nc.vector.tensor_tensor(walk_dst(rounded[h]), walk_src(vals[:, :, HALF * h : HALF * (h + 1)]), factor, ALU.mult)
+                cols = slice(HALF * h, HALF * (h + 1))
+                nc.vector.tensor_tensor(walk_dst(rounded[h]), walk_src(first[:, :, cols]), walk_src(second[:, :, cols]), op)
             for h in range(2):
                 cols = slice(HALF * h, HALF * (h + 1))
                 nc.vector.quantize_mx(codes[:, cols].bitcast(FP8X4), scales[:, cols], rounded[h])
@@ -187,61 +201,77 @@ def tile_picked_fkcdnormbgapgmid_none_po_kernel(
             extremes(t, mb)
             combine(t)
             mb = ahead
-        for t in range(PACK):
-            scalar_gather(at_n2[:, t, :], y[t][:], n2_l[:])
-            scalar_gather(at_n1[:, t, :], y[t][:], n1_l[:])
-        z2_q, z2_s = quantise(u, gs_t, "z2")
+        for first in (0, HALF):
+            cols = slice(first, first + HALF)
+            for t in range(PACK):
+                scalar_gather(at_n2[:, t, cols], gained[t][:], half_list(n2_l, cols))
+                scalar_gather(at_n1[:, t, cols], gained[t][:], half_list(n1_l, cols))
+        z2_q, z2_s = quantise(u[:], gs_t[:].unsqueeze(2).to_broadcast([P, PACK, S]), ALU.mult, "z2")
 
         size = keep.tile([P, PACK, S], F32, name="size")
         for t in range(PACK):
             acc = product(t, xc[:, P * t : P * (t + 1)].bitcast(FP8X4), xc_s, z2_q, z2_s)
             nc.scalar.activation(size[:, t, :], acc[:], ACT.Abs, scale=0.0625)
-        for t in range(PACK):
-            nc.vector.tensor_tensor(d[:, t, :], at_n1[:, t, :], at_n2[:, t, :], ALU.subtract)
-        z_q, z_s = quantise(d, gn_t, "z")
+        z_q, z_s = quantise(at_n1[:], at_n2[:], ALU.subtract, "z")
 
         out_rows = out_0.rearrange("(p t) j -> p t j", t=PACK)
         codes = keep.tile([P, S], U32, name="codes", align_bytes=64)
         scales = keep.tile([P, S], U8, name="scales", align_bytes=64)
         out_words = out_1[0].rearrange("p j t -> p (j t)").bitcast(I32)
-        chunks = [slice(c, c + CHUNK) for c in range(0, S, CHUNK)]
-
+        chunks = [slice(sum(WIDTHS[:c]), sum(WIDTHS[: c + 1])) for c in range(len(WIDTHS))]
         at_n5 = keep.tile([P, PACK, S], F32, name="at_n5")
-        for cols in chunks:
-            for t in range(PACK):
-                gather = vector_gather if t < N5_ON_VECTOR else scalar_gather
-                gather(at_n5[:, t, cols], size[:, t, :], half_list(n5_l, cols))
+        inv = keep.tile([P, PACK, S], F32, name="inv")
         a = keep.tile([P, PACK, S], F32, name="a")
-        for t in range(PACK):
-            acc = product(t, fp4_cols(w2_q, t), w2_s, z_q, z_s)
-            nc.scalar.copy(a[:, t, :], acc[:])
 
-        def parts(cols):
-            den = ring.tile([P, PACK, CHUNK], F32, name="den")
-            nc.vector.tensor_tensor(den[:], at_n5[:, :, cols], size[:, :, cols], ALU.add)
-            at_n4 = ring.tile([P, PACK, CHUNK], F32, name="at_n4")
+        def fetch_sizes(c):
+            cols = chunks[c]
             for t in range(PACK):
-                gather = vector_gather if t < N4_ON_VECTOR else scalar_gather
-                gather(at_n4[:, t, :], a[:, t, :], half_list(n4_l, cols))
-            root = ring.tile([P, PACK, CHUNK], F32, name="root")
-            nc.scalar.activation(root[:], den[:], ACT.Abs_reciprocal_sqrt, bias=0.5)
-            inv = ring.tile([P, PACK, CHUNK], F32, name="inv")
-            nc.scalar.activation(inv[:], root[:], ACT.Square)
-            num = ring.tile([P, PACK, CHUNK], F32, name="num")
-            nc.vector.tensor_tensor(num[:], a[:, :, cols], at_n4[:], ALU.subtract)
-            return num, inv
+                gather = vector_gather if t < N5_ON_VECTOR[c] else scalar_gather
+                gather(at_n5[:, t, cols], size[:, t, :], half_list(n5_l, cols))
 
-        def finish(cols, num, inv):
-            res = keep.tile([P, PACK, CHUNK], F32, name=f"res{cols.start}")
-            nc.vector.tensor_tensor(res[:], num[:], inv[:], ALU.mult)
+        def inverse(cols):
+            width = cols.stop - cols.start
+            den = ring.tile([P, PACK, width], F32, name="den")
+            nc.vector.tensor_tensor(den[:], at_n5[:, :, cols], size[:, :, cols], ALU.add)
+            root = ring.tile([P, PACK, width], F32, name="root")
+            nc.scalar.activation(root[:], den[:], ACT.Abs_reciprocal_sqrt, bias=0.5)
+            nc.scalar.activation(inv[:, :, cols], root[:], ACT.Square)
+
+        def fetch_a(c):
+            width = WIDTHS[c]
+            at_n4 = ring.tile([P, PACK, width], F32, name="at_n4")
+            for t in range(PACK):
+                gather = vector_gather if t < N4_ON_VECTOR[c] else scalar_gather
+                gather(at_n4[:, t, :], a[:, t, :], half_list(n4_l, chunks[c]))
+            return at_n4
+
+        def finish(cols, at_n4):
+            width = cols.stop - cols.start
+            num = ring.tile([P, PACK, width], F32, name="num")
+            nc.vector.tensor_tensor(num[:], a[:, :, cols], at_n4[:], ALU.subtract)
+            res = keep.tile([P, PACK, width], F32, name=f"res{cols.start}")
+            nc.vector.tensor_tensor(res[:], num[:], inv[:, :, cols], ALU.mult)
             nc.sync.dma_start(out_rows[:, :, cols], res[:])
-            grouped = ring.tile([P, CHUNK * PACK], BF16, name="grouped", align_bytes=64)
+            grouped = ring.tile([P, width * PACK], BF16, name="grouped", align_bytes=64)
             nc.vector.tensor_copy(walk_dst(grouped[:]), walk_src(res[:]))
             nc.vector.quantize_mx(codes[:, cols].bitcast(FP8X4), scales[:, cols], grouped[:])
             nc.sync.dma_start(out_words[:, cols], codes[:, cols].bitcast(I32))
 
-        for cols in chunks:
-            finish(cols, *parts(cols))
+        for c, cols in enumerate(chunks):
+            fetch_sizes(c)
+            if 1 <= c <= LEAD:
+                inverse(chunks[c - 1])
+        for t in range(PACK):
+            acc = product(t, fp4_cols(w2_q, t), w2_s, z_q, z_s)
+            if t < PACK - A_ON_SCALAR:
+                nc.vector.tensor_copy(a[:, t, :], acc[:])
+            else:
+                nc.scalar.copy(a[:, t, :], acc[:])
+        for c, cols in enumerate(chunks):
+            at_n4 = fetch_a(c)
+            if c + LEAD < len(chunks):
+                inverse(chunks[c + LEAD])
+            finish(cols, at_n4)
         for q in range(4):
             queue = nc.sync if q % 2 == 0 else nc.scalar
             queue.dma_start(out_2[0, 4 * q : 4 * q + 4, :].bitcast(I32), scales[32 * q : 32 * q + 4, :].bitcast(I32))

@@ -83,8 +83,8 @@ def tile_picked_fkcdnormbgapgmid_none_po_kernel(
             return lst[:, first // LANES : (first + count) // LANES]
 
         offs_l = load_list(offs, "offs_l")
-        xs = load_scales_everywhere(x_scales, "xs")
         w1_raw = load_words(w1_words[0], "w1_raw", nc.sync)
+        xs = load_scales_everywhere(x_scales, "xs")
         cand_l = load_list(cand, "cand_l")
         xw = keep.tile([P, T], I32, name="xw", align_bytes=64)
         nc.sync.dma_start(xw[:], x_words[0].rearrange("p n t -> p (n t)").bitcast(I32))
@@ -103,7 +103,11 @@ def tile_picked_fkcdnormbgapgmid_none_po_kernel(
         for t in range(PACK):
             nc.gpsimd.memset(y[t][:, S:], 0.0)
 
-        w1_q = deal(nc.gpsimd, w1_raw[:], "w1_q", U8, 2, 8)
+        warm = keep.tile([P, 2], F32, name="warm")
+        nc.gpsimd.memset(warm[:, 0:1], 1.0)
+        nc.scalar.activation(warm[:, 1:2], warm[:, 0:1], ACT.Abs_reciprocal_sqrt, bias=0.5)
+
+        w1_q = deal(nc.vector, w1_raw[:], "w1_q", U8, 2, 8)
         xq_s = keep.tile([P, S], U8, name="xq_s", align_bytes=64)
         nc.vector.tensor_copy(xq_s[:], xs[:].indirect(offs_l[:]))
         xc_s_raw = keep.tile([P, C], U8, name="xc_s_raw", align_bytes=64)

from contextlib import ExitStack

import concourse.mybir as mybir

K, T, S, H, N, C, MEMBERS = 512, 2048, 512, 512, 512, 512, 4
FLOPS = 2 * K * H * S + 2 * H * N * S + 2 * K * C * S

F32 = mybir.dt.float32
BF16 = mybir.dt.bfloat16
I32 = mybir.dt.int32
U32 = mybir.dt.uint32
U16 = mybir.dt.uint16
U8 = mybir.dt.uint8
FP8X4 = mybir.dt.float8_e4m3fn_x4
FP4X4 = mybir.dt.float4_e2m1fn_x4
ALU = mybir.AluOpType
ACT = mybir.ActivationFunctionType

P = 128
PACK = 4
LANES = 16
SPARE = 16
HALF = S // 2
WIDTHS = (128, 128, 128, 128)
A_ON_SCALAR = 0
LEAD = 1
N5_ON_VECTOR = (4, 0, 0, 0)
N4_ON_VECTOR = (4, 0, 0, 0)
MEMBERS_ON_VECTOR = (2, 0, 0, 0)


def tile_picked_fkcdnormbgapgmid_none_po_kernel(
    tc, x_words, x_scales, w1_words, w1_scales, gn, w2_words, w2_scales, gs, offs, n1, n2, n3, cand, n4, n5, out_0, out_1, out_2
):
    nc = tc.nc
    with ExitStack() as ctx:
        keep = ctx.enter_context(tc.tile_pool(name="keep", bufs=1))
        ring = ctx.enter_context(tc.tile_pool(name="ring", bufs=2))
        psum = ctx.enter_context(tc.psum_pool(name="psum", bufs=8))

        def load_list(src, name):
            lst = keep.tile([P, src.shape[1]], U16, name=name)
            nc.sync.dma_start(lst[:], src)
            return lst

        def load_scales(src, name, clearers, queue):
            width = src.shape[2]
            plane = keep.tile([P, width], U8, name=name, align_bytes=64)
            share = width // len(clearers)
            for e, engine in enumerate(clearers):
                engine.memset(plane[:, share * e : share * (e + 1)].bitcast(I32), 0)
            for q in range(4):
                queue.dma_start(plane[32 * q : 32 * q + 4, :].bitcast(I32), src[0, 4 * q : 4 * q + 4, :].bitcast(I32))
            return plane

        def load_scales_everywhere(src, name):
            width = src.shape[2]
            plane = keep.tile([P, width], U8, name=name, align_bytes=64)
            for q in range(4):
                rows = src[0, 4 * q : 4 * q + 4, :].bitcast(I32).unsqueeze(0).to_broadcast([8, 4, width // 4])
                nc.sync.dma_start(plane[32 * q : 32 * q + 32, :].bitcast(I32), rows)
            return plane

        def load_words(src2d, name, queue):
            raw = keep.tile([P, src2d.shape[1]], U8, name=name, align_bytes=64)
            queue.dma_start(raw[:].bitcast(I32), src2d.bitcast(I32))
            return raw

        def load_gain(src, name):
            gain = keep.tile([P, PACK], F32, name=name)
            nc.sync.dma_start(gain[:], src.rearrange("(p t) o -> p (t o)", t=PACK))
            return gain

        def deal(engine, src, name, dtype, unit, run):
            dealt = keep.tile([P, src.shape[1]], dtype, name=name, align_bytes=64)
            engine.tensor_copy(
                dealt[:].rearrange("p (t c i b) -> p c t i b", t=PACK, i=run, b=unit),
                src.rearrange("p (c i t b) -> p c t i b", t=PACK, i=run, b=unit),
            )
            return dealt

        def entries(lst, first, count):
            return lst[:, first // LANES : (first + count) // LANES]

        offs_l = load_list(offs, "offs_l")
        w1_raw = load_words(w1_words[0], "w1_raw", nc.sync)
        xs = load_scales_everywhere(x_scales, "xs")
        cand_l = load_list(cand, "cand_l")
        xw = keep.tile([P, T], I32, name="xw", align_bytes=64)
        nc.sync.dma_start(xw[:], x_words[0].rearrange("p n t -> p (n t)").bitcast(I32))
        w1s_raw = load_scales(w1_scales, "w1s_raw", (nc.gpsimd,), nc.sync)
        n3_l = load_list(n3, "n3_l")
        gn_t = load_gain(gn, "gn_t")
        w2_raw = load_words(w2_words[0], "w2_raw", nc.sync)
        w2s_raw = load_scales(w2_scales, "w2s_raw", (nc.gpsimd,), nc.sync)
        n2_l = load_list(n2, "n2_l")
        n1_l = load_list(n1, "n1_l")
        gs_t = load_gain(gs, "gs_t")
        n5_l = load_list(n5, "n5_l")
        n4_l = load_list(n4, "n4_l")

        y = [keep.tile([P, S + SPARE], F32, name=f"y{t}") for t in range(PACK)]
        for t in range(PACK):
            nc.gpsimd.memset(y[t][:, S:], 0.0)

        warm = keep.tile([P, 2], F32, name="warm")
        nc.gpsimd.memset(warm[:, 0:1], 1.0)
        nc.scalar.activation(warm[:, 1:2], warm[:, 0:1], ACT.Abs_reciprocal_sqrt, bias=0.5)

        w1_q = deal(nc.vector, w1_raw[:], "w1_q", U8, 2, 8)
        xq_s = keep.tile([P, S], U8, name="xq_s", align_bytes=64)
        nc.vector.tensor_copy(xq_s[:], xs[:].indirect(offs_l[:]))
        xc_s_raw = keep.tile([P, C], U8, name="xc_s_raw", align_bytes=64)
        nc.vector.tensor_copy(xc_s_raw[:], xs[:].indirect(cand_l[:]))
        xq = keep.tile([P, S], U32, name="xq", align_bytes=64)
        for first in (0, HALF):
            nc.vector.tensor_copy(xq[:, first : first + HALF], xw[:].bitcast(U32).indirect(entries(offs_l, first, HALF)))
        w1_s = deal(nc.gpsimd, w1s_raw[:], "w1_s", U8, 1, 16)
        xc_s = deal(nc.vector, xc_s_raw[:], "w1s_raw", U8, 1, 16)
        w2_q = deal(nc.gpsimd, w2_raw[:], "w2_q", U8, 2, 8)
        w2_s = deal(nc.gpsimd, w2s_raw[:], "w2_s", U8, 1, 16)

        def product(t, lhs, lhs_s, rhs, rhs_s, cols=slice(0, S)):
            acc = psum.tile([P, cols.stop - cols.start], F32, name="acc")
            nc.tensor.matmul_mx(acc[:], lhsT=lhs, lhsT_scale=lhs_s[:, P * t : P * (t + 1)], rhs=rhs[:, cols].bitcast(FP8X4), rhs_scale=rhs_s[:, cols], start=True, stop=True)
            return acc

        def fp4_cols(w, t):
            return w[:, 2 * P * t : 2 * P * (t + 1)].bitcast(FP4X4)

        for first in (0, HALF):
            cols = slice(first, first + HALF)
            acc = product(0, fp4_cols(w1_q, 0), w1_s, xq, xq_s, cols)
            nc.scalar.copy(y[0][:, cols], acc[:])
        for t in range(1, PACK):
            acc = product(t, fp4_cols(w1_q, t), w1_s, xq, xq_s)
            nc.vector.tensor_copy(y[t][:, :S], acc[:])
        gained = [keep.tile([P, S + SPARE], F32, name=f"gained{t}") for t in range(PACK)]
        for t in range(PACK):
            nc.gpsimd.tensor_scalar(gained[t][:], y[t][:], gn_t[:, t : t + 1], 0.0, ALU.mult, ALU.add)

        def scalar_gather(dst, window, offsets):
            nc.scalar.activation(dst, window.indirect(offsets), ACT.Copy)

        def vector_gather(dst, window, offsets):
            nc.vector.tensor_copy(dst, window.indirect(offsets))

        def fetch_members(t):
            mb = keep.tile([P, S, MEMBERS], F32, name=f"mb{t}")
            flat = mb[:].rearrange("p j m -> p (j m)")
            for piece in range(MEMBERS):
                gather = vector_gather if piece >= MEMBERS - MEMBERS_ON_VECTOR[t] else scalar_gather
                gather(flat[:, S * piece : S * (piece + 1)], y[t][:], entries(n3_l, S * piece, S))
            return mb

        u = keep.tile([P, PACK, S], F32, name="u")
        lo = keep.tile([P, S, 2], F32, name="lo", align_bytes=64)
        hi = keep.tile([P, S, 2], F32, name="hi", align_bytes=64)
        mn = keep.tile([P, S], F32, name="mn")
        mx = keep.tile([P, S], F32, name="mx")
        top = keep.tile([P, S], F32, name="top")

        def extremes(t, mb):
            nc.vector.tensor_tensor(lo[:], mb[:, :, 0:2], mb[:, :, 2:4], ALU.min)
            nc.vector.tensor_tensor(hi[:], mb[:, :, 0:2], mb[:, :, 2:4], ALU.max)
            nc.vector.tensor_tensor(mn[:], lo[:, :, 0], lo[:, :, 1], ALU.min)
            nc.vector.tensor_tensor(mx[:], hi[:, :, 0], hi[:, :, 1], ALU.max)
            nc.vector.tensor_tensor(top[:], mn[:], y[t][:, :S], ALU.max)

        def combine(t):
            nc.vector.scalar_tensor_tensor(u[:, t, :], mx[:], -0.5, top[:], ALU.mult, ALU.add)

        def walk_src(ap):
            return ap.rearrange("p t (c i) -> p c t i", i=2)

        def walk_dst(ap):
            return ap.rearrange("p (c i t) -> p c t i", i=2, t=PACK)

        def quantise(first, second, op, name):
            codes = keep.tile([P, S], U32, name=name + "_q", align_bytes=64)
            scales = keep.tile([P, S], U8, name=name + "_s", align_bytes=64)
            rounded = [pairs[:].rearrange("p j m -> p (j m)").bitcast(BF16)[:, : HALF * PACK] for pairs in (lo, hi)]
            for h in range(2):
                cols = slice(HALF * h, HALF * (h + 1))
                nc.vector.tensor_tensor(walk_dst(rounded[h]), walk_src(first[:, :, cols]), walk_src(second[:, :, cols]), op)
            for h in range(2):
                cols = slice(HALF * h, HALF * (h + 1))
                nc.vector.quantize_mx(codes[:, cols].bitcast(FP8X4), scales[:, cols], rounded[h])
            return codes, scales

        mb0 = fetch_members(0)
        xc_raw = keep.tile([P, C], U32, name="xc_raw", align_bytes=64)
        nc.vector.tensor_copy(xc_raw[:], xw[:].bitcast(U32).indirect(cand_l[:]))
        xc = deal(nc.vector, xc_raw[:].bitcast(I32), "xc", I32, 1, 4)

        at_n2 = keep.tile([P, PACK, S], F32, name="at_n2")
        at_n1 = keep.tile([P, PACK, S], F32, name="at_n1")

        def half_list(lst, cols):
            return entries(lst, cols.start, cols.stop - cols.start)

        mb = mb0
        for t in range(PACK):
            ahead = fetch_members(t + 1) if t + 1 < PACK else None
            extremes(t, mb)
            combine(t)
            mb = ahead
        for first in (0, HALF):
            cols = slice(first, first + HALF)
            for t in range(PACK):
                scalar_gather(at_n2[:, t, cols], gained[t][:], half_list(n2_l, cols))
                scalar_gather(at_n1[:, t, cols], gained[t][:], half_list(n1_l, cols))
        z2_q, z2_s = quantise(u[:], gs_t[:].unsqueeze(2).to_broadcast([P, PACK, S]), ALU.mult, "z2")

        size = keep.tile([P, PACK, S], F32, name="size")
        for t in range(PACK):
            acc = product(t, xc[:, P * t : P * (t + 1)].bitcast(FP8X4), xc_s, z2_q, z2_s)
            nc.scalar.activation(size[:, t, :], acc[:], ACT.Abs, scale=0.0625)
        z_q, z_s = quantise(at_n1[:], at_n2[:], ALU.subtract, "z")

        out_rows = out_0.rearrange("(p t) j -> p t j", t=PACK)
        codes = keep.tile([P, S], U32, name="codes", align_bytes=64)
        scales = keep.tile([P, S], U8, name="scales", align_bytes=64)
        out_words = out_1[0].rearrange("p j t -> p (j t)").bitcast(I32)
        chunks = [slice(sum(WIDTHS[:c]), sum(WIDTHS[: c + 1])) for c in range(len(WIDTHS))]
        at_n5 = keep.tile([P, PACK, S], F32, name="at_n5")
        inv = keep.tile([P, PACK, S], F32, name="inv")
        a = keep.tile([P, PACK, S], F32, name="a")

        def fetch_sizes(c):
            cols = chunks[c]
            for t in range(PACK):
                gather = vector_gather if t < N5_ON_VECTOR[c] else scalar_gather
                gather(at_n5[:, t, cols], size[:, t, :], half_list(n5_l, cols))

        def inverse(cols):
            width = cols.stop - cols.start
            den = ring.tile([P, PACK, width], F32, name="den")
            nc.vector.tensor_tensor(den[:], at_n5[:, :, cols], size[:, :, cols], ALU.add)
            root = ring.tile([P, PACK, width], F32, name="root")
            nc.scalar.activation(root[:], den[:], ACT.Abs_reciprocal_sqrt, bias=0.5)
            nc.scalar.activation(inv[:, :, cols], root[:], ACT.Square)

        def fetch_a(c):
            width = WIDTHS[c]
            at_n4 = ring.tile([P, PACK, width], F32, name="at_n4")
            for t in range(PACK):
                gather = vector_gather if t < N4_ON_VECTOR[c] else scalar_gather
                gather(at_n4[:, t, :], a[:, t, :], half_list(n4_l, chunks[c]))
            return at_n4

        def finish(cols, at_n4):
            width = cols.stop - cols.start
            num = ring.tile([P, PACK, width], F32, name="num")
            nc.vector.tensor_tensor(num[:], a[:, :, cols], at_n4[:], ALU.subtract)
            res = keep.tile([P, PACK, width], F32, name=f"res{cols.start}")
            nc.vector.tensor_tensor(res[:], num[:], inv[:, :, cols], ALU.mult)
            nc.sync.dma_start(out_rows[:, :, cols], res[:])
            grouped = ring.tile([P, width * PACK], BF16, name="grouped", align_bytes=64)
            nc.vector.tensor_copy(walk_dst(grouped[:]), walk_src(res[:]))
            nc.vector.quantize_mx(codes[:, cols].bitcast(FP8X4), scales[:, cols], grouped[:])
            nc.sync.dma_start(out_words[:, cols], codes[:, cols].bitcast(I32))

        for c, cols in enumerate(chunks):
            fetch_sizes(c)
            if 1 <= c <= LEAD:
                inverse(chunks[c - 1])
        for t in range(PACK):
            acc = product(t, fp4_cols(w2_q, t), w2_s, z_q, z_s)
            if t < PACK - A_ON_SCALAR:
                nc.vector.tensor_copy(a[:, t, :], acc[:])
            else:
                nc.scalar.copy(a[:, t, :], acc[:])
        for c, cols in enumerate(chunks):
            at_n4 = fetch_a(c)
            if c + LEAD < len(chunks):
                inverse(chunks[c + LEAD])
            finish(cols, at_n4)
        for q in range(4):
            queue = nc.sync if q % 2 == 0 else nc.scalar
            queue.dma_start(out_2[0, 4 * q : 4 * q + 4, :].bitcast(I32), scales[32 * q : 32 * q + 4, :].bitcast(I32))
